import numpy as np
import ml_dtypes


def mxq(x, axis, fmt="e4m3"):
    dtype, down = {"e4m3": (ml_dtypes.float8_e4m3fn, 7), "e5m2": (ml_dtypes.float8_e5m2, 14)}[fmt]
    v = np.moveaxis(np.asarray(x, np.float32).astype(ml_dtypes.bfloat16).astype(np.float64), axis, -1)
    blocks = v.reshape(v.shape[:-1] + (-1, 32))
    amax = np.abs(blocks).max(-1, keepdims=True)
    byte = np.maximum(np.where(amax > 0, np.frexp(amax)[1] - 1 + 127, 0) - down, 1)
    scale = np.exp2(byte - 127.0)
    codes = (blocks / scale).astype(np.float32).astype(dtype).astype(np.float64)
    return np.moveaxis((codes * scale).reshape(v.shape), -1, axis)


WIDE = False


def mx_kscale(k):
    if not WIDE:
        return np.ones(k)
    levels = np.array([10, -10, 5, -5, 0])
    if k % 512:
        return np.exp2(np.random.permutation(np.resize(levels, k // 32))).repeat(32)
    a = np.empty((k // 512, 16))
    for p in range(k // 512):
        a[p, :8] = np.random.permutation(np.resize(levels, 8))
        for g in range(8):
            far = levels[np.abs(levels - a[p, g]) >= 10]
            a[p, g + 8] = far[np.random.randint(len(far))]
    return np.exp2(a.ravel()).repeat(32)


def f64(x):
    return np.asarray(x).astype(np.float64)


def striped(idx):
    return np.tile(np.asarray(idx).reshape(-1, 16).T, (8, 1)).astype(np.uint16)


def unstriped(offs):
    return offs[:16].T.reshape(-1).astype(np.int64)


E2M1 = np.array([0.0, 0.5, 1.0, 1.5, 2.0, 3.0, 4.0, 6.0, -0.0, -0.5, -1.0, -1.5, -2.0, -3.0, -4.0, -6.0])


def pack_weight(w, fmt):
    k, n = w.shape
    w = f64(np.asarray(w, np.float32).astype(ml_dtypes.bfloat16)).reshape(k // 32, 32, n)
    amax = np.abs(w).max(1)
    if fmt == "e4m3":
        byte = np.frexp(amax)[1] - 1 + 127 - 7
    else:
        mant, ex = np.frexp(amax / 6.0)
        byte = np.where(mant > 0.5, ex, ex - 1) + 127
    byte = np.clip(np.where(amax > 0, byte, 1), 1, 254)
    scaled = (w * np.exp2(127.0 - byte)[:, None, :]).reshape(k, n).astype(np.float32)
    by_word = np.ascontiguousarray(scaled.reshape(k // 512, 128, 4, n).transpose(0, 1, 3, 2))
    if fmt == "e4m3":
        words = by_word.astype(ml_dtypes.float8_e4m3fn).view(np.uint8)
    else:
        c = by_word.astype(ml_dtypes.float4_e2m1fn).view(np.uint8) & 0xF
        words = (c[..., 0::2] | (c[..., 1::2] << 4)).reshape(k // 512, 128, 2 * n)
    return np.ascontiguousarray(words), np.ascontiguousarray(byte.astype(np.uint8).reshape(k // 512, 16, n))


def unpack_weight(words, scales, fmt):
    g, _, n = scales.shape
    words = np.ascontiguousarray(words).reshape(g, 128, n, -1)
    if fmt == "e4m3":
        vals = words.view(ml_dtypes.float8_e4m3fn).astype(np.float64)
    else:
        nib = np.empty((g, 128, n, 4), np.uint8)
        nib[..., 0::2] = words & 0xF
        nib[..., 1::2] = words >> 4
        vals = E2M1[nib]
    vals = vals * np.repeat(np.exp2(scales.astype(np.float64) - 127.0), 8, axis=1)[..., None]
    return vals.transpose(0, 1, 3, 2).reshape(g * 512, n)


K, T, J, N, M = 1024, 1024, 512, 512, 512


def setup_inputs():
    n = np.random.standard_normal
    idx = np.random.permutation(T)[:J]
    fk = mx_kscale(K)
    ft = mx_kscale(T)
    xtp = pack_weight(n((K, J)) / fk[:, None], "e4m3")
    wp = pack_weight(n((K, N)) * 1 / np.sqrt(K) * fk[:, None], "e2m1")
    kyp = pack_weight(n((T, M)) * 1 / np.sqrt(T) * ft[:, None], "e4m3")
    return {
        "xt_words": xtp[0],
        "xt_scales": xtp[1],
        "w_words": wp[0],
        "w_scales": wp[1],
        "old": (1.0 * n((N, T))).astype(np.float32),
        "ct1": (np.random.uniform(0.5, 2.0, (T, 1)) / ft[:, None]).astype(np.float32),
        "ky_words": kyp[0],
        "ky_scales": kyp[1],
        "offs": striped(idx),
    }


def reference(xt_words, xt_scales, w_words, w_scales, old, ct1, ky_words, ky_scales, offs):
    idx = unstriped(offs)
    xtu = unpack_weight(xt_words, xt_scales, "e4m3")
    wu = unpack_weight(w_words, w_scales, "e2m1")
    kyu = unpack_weight(ky_words, ky_scales, "e4m3")
    p = wu.T @ xtu
    pp = np.zeros((N, T))
    pp[:, idx] = p
    pg = pp + 0.5 * f64(old)
    pt = pg.T
    pw = pt * f64(ct1)
    pwq = mxq(pw, 0, "e4m3")
    y = pwq.T @ kyu
    return y

from contextlib import ExitStack

import concourse.mybir as mybir
from concourse.masks import make_identity

K, T, J, N, M = 1024, 1024, 512, 512, 512
FLOPS = 2 * K * N * J + 2 * T * N * M

F32 = mybir.dt.float32
BF16 = mybir.dt.bfloat16
I32 = mybir.dt.int32
U32 = mybir.dt.uint32
U16 = mybir.dt.uint16
U8 = mybir.dt.uint8
FP8X4 = mybir.dt.float8_e4m3fn_x4
FP4X4 = mybir.dt.float4_e2m1fn_x4
COPY = mybir.ActivationFunctionType.Copy
MULT = mybir.AluOpType.mult

P = 128
PACK = 4
PASSES = 2
BLOCKS = N // P
HEAD = 128
SCALAR_BLOCKS = 2


def load_scale_rows(queues, plane, scales):
    for r in range(4):
        queues[r].dma_start(
            out=plane[r:P:32, :, :].bitcast(I32),
            in_=scales[:, r:16:4, :].rearrange("z q c -> q z c").bitcast(I32),
        )


def tile_moe_expert_page_to_keys_kernel(
    tc, xt_words, xt_scales, w_words, w_scales, old, ct1, ky_words, ky_scales, offs, out
):
    nc = tc.nc
    with ExitStack() as ctx:
        keep = ctx.enter_context(tc.tile_pool(name="keep", bufs=1))
        psum = ctx.enter_context(tc.psum_pool(name="psum", bufs=1))

        def bank(i, cols, name):
            return psum.tile([P, cols], F32, tag="bank%d" % i, name=name)

        xt_plane = keep.tile([P, PASSES, J], U8, align_bytes=64)
        w_plane = keep.tile([P, PASSES, N], U8, align_bytes=64)
        ky_plane = keep.tile([P, PASSES, M], U8, align_bytes=64)
        xt = keep.tile([P, PASSES, J], U32, align_bytes=64)
        w_head = keep.tile([P, PASSES, 2 * P], U8, align_bytes=64)
        w_rest = keep.tile([P, PASSES, 2 * (N - P)], U8, align_bytes=64)
        ky = keep.tile([P, PASSES, M], U32, align_bytes=64)
        offsets = keep.tile([P, J // 16], U16)
        ct = keep.tile([P, PASSES, PACK], F32)
        ident = keep.tile([P, P], F32)
        windows = [keep.tile([P, T], F32, name="window%d" % b) for b in range(BLOCKS)]
        olds = [keep.tile([P, T], F32, name="old%d" % b) for b in range(BLOCKS)]

        nc.vector.memset(xt_plane[:].rearrange("p z c -> p (z c)").bitcast(I32), 0)
        nc.vector.memset(w_plane[:].rearrange("p z c -> p (z c)").bitcast(I32), 0)

        xt_rows = xt_words.rearrange("z p c r -> p z (c r)")
        w_rows = w_words.rearrange("z p c -> p z c")
        nc.sync.dma_start(out=xt[:, :, 0:HEAD].bitcast(I32), in_=xt_rows[:, :, 0 : 4 * HEAD].bitcast(I32))
        nc.scalar.dma_start(out=w_head[:].bitcast(I32), in_=w_rows[:, :, 0 : 2 * P].bitcast(I32))
        load_scale_rows([nc.sync] * 4, xt_plane, xt_scales)
        load_scale_rows([nc.scalar, nc.scalar, nc.sync, nc.sync], w_plane, w_scales)
        nc.sync.dma_start(offsets[:], offs)
        nc.sync.dma_start(out=xt[:, :, HEAD:J].bitcast(I32), in_=xt_rows[:, :, 4 * HEAD : 4 * J].bitcast(I32))
        nc.sync.dma_start(out=w_rest[:].bitcast(I32), in_=w_rows[:, :, 2 * P : 2 * N].bitcast(I32))
        for b in range(BLOCKS):
            nc.sync.dma_start(out=olds[b][:], in_=old[b * P : (b + 1) * P, :])
        nc.sync.dma_start(out=ct[:], in_=ct1.rearrange("(z p r) o -> p z (r o)", z=PASSES, r=PACK))
        nc.gpsimd.memset(ky_plane[:].rearrange("p z c -> p (z c)").bitcast(I32), 0)
        nc.sync.dma_start(out=ky[:].bitcast(I32), in_=ky_words.rearrange("z p c r -> p z (c r)").bitcast(I32))
        load_scale_rows([nc.sync] * 4, ky_plane, ky_scales)

        for b in range(BLOCKS):
            nc.vector.memset(windows[b][:], 0.0)
        make_identity(nc, ident[:])

        def expert(acc, b, j0, j1):
            for z in range(PASSES):
                if b == 0:
                    words = w_head[:, z, :]
                else:
                    words = w_rest[:, z, 2 * P * (b - 1) : 2 * P * b]
                nc.tensor.matmul_mx(
                    out=acc,
                    lhsT=words.bitcast(FP4X4),
                    lhsT_scale=w_plane[:, z, b * P : (b + 1) * P],
                    rhs=xt[:, z, j0:j1].bitcast(FP8X4),
                    rhs_scale=xt_plane[:, z, j0:j1],
                    start=(z == 0),
                    stop=(z == PASSES - 1),
                )

        def scatter(b, acc, j0, j1, name):
            slots = keep.tile([P, j1 - j0], F32, name=name)
            nc.scalar.copy(out=slots[:], in_=acc)
            nc.vector.tensor_copy(windows[b][:].indirect(offsets[:, j0 // 16 : j1 // 16]), slots[:])

        acc = bank(6, HEAD, "p_head")
        expert(acc[:], 0, 0, HEAD)
        scatter(0, acc[:], 0, HEAD, "slots_head")
        acc = bank(7, J - HEAD, "p_0")
        for j0 in range(HEAD, J, P):
            expert(acc[:, j0 - HEAD : j0 - HEAD + P], 0, j0, j0 + P)
        scatter(0, acc[:], HEAD, J, "slots0")
        for b in range(1, BLOCKS):
            acc = bank(2 + b, J, "p_%d" % b)
            expert(acc[:], b, 0, J)
            scatter(b, acc[:], 0, J, "slots%d" % b)

        turned = []
        for b in range(BLOCKS):
            half_old = keep.tile([P, PASSES, PACK, P], F32, name="half_old%d" % b)
            nc.scalar.activation(
                out=half_old[:].rearrange("p z r q -> p z q r"),
                in_=olds[b][:].rearrange("p (z q r) -> p z q r", z=PASSES, r=PACK),
                func=COPY,
                scale=0.5,
            )
            pair = [bank(2 * b + z, PACK * P, "turned%d_%d" % (b, z)) for z in range(PASSES)]
            for z in range(PASSES):
                for r in range(PACK):
                    nc.tensor.matmul(
                        pair[z][:, r * P : (r + 1) * P], half_old[:, z, r, :], ident[:],
                        start=(r == 0), stop=False, is_transpose=True,
                    )
            for z in range(PASSES):
                for r in range(PACK):
                    nc.tensor.matmul(
                        pair[z][:, r * P : (r + 1) * P],
                        windows[b][:, 512 * z + r : 512 * (z + 1) : PACK], ident[:],
                        start=False, stop=(r == PACK - 1), is_transpose=True,
                    )
            turned.append(pair)

        def weigh(b):
            woven = keep.tile([P, PASSES, P * PACK], BF16, name="woven%d" % b,
                              tag="woven%d" % (1 if b == 3 else b), align_bytes=64)
            for z in range(PASSES):
                if b < SCALAR_BLOCKS:
                    planes = keep.tile([P, PACK, P], BF16, name="planes%d_%d" % (b, z))
                    for r in range(PACK):
                        nc.scalar.activation(
                            out=planes[:, r, :], in_=turned[b][z][:, r * P : (r + 1) * P],
                            func=COPY, scale=ct[:, z, r : r + 1],
                        )
                    nc.scalar.copy(
                        out=woven[:, z, :].rearrange("p (c i r) -> p c r i", i=4, r=PACK),
                        in_=planes[:].rearrange("p r (c i) -> p c r i", i=4),
                    )
                else:
                    nc.vector.tensor_tensor(
                        out=woven[:, z, :].rearrange("p (n r) -> p n r", r=PACK),
                        in0=turned[b][z][:].rearrange("p (r n) -> p n r", r=PACK),
                        in1=ct[:, z : z + 1, :].to_broadcast([P, P, PACK]),
                        op=MULT,
                    )
            return woven

        def finish(b, woven):
            codes = keep.tile([P, PASSES * P], U32, name="codes%d" % b, align_bytes=64)
            plane = keep.tile([P, PASSES * P], U8, name="plane%d" % b, align_bytes=64)
            nc.vector.quantize_mx(
                out=codes[:].bitcast(FP8X4), scales=plane[:], in_=woven[:].rearrange("p z c -> p (z c)")
            )
            pieces = [(2 * b, 0, M)] if b < BLOCKS - 1 else [(1, 0, M // 2), (3, M // 2, M)]
            for i, m0, m1 in pieces:
                acc = bank(i, m1 - m0, "out%d_%d" % (b, m0))
                for z in range(PASSES):
                    nc.tensor.matmul_mx(
                        out=acc[:],
                        lhsT=codes[:, z * P : (z + 1) * P].bitcast(FP8X4),
                        lhsT_scale=plane[:, z * P : (z + 1) * P],
                        rhs=ky[:, z, m0:m1].bitcast(FP8X4),
                        rhs_scale=ky_plane[:, z, m0:m1],
                        start=(z == 0),
                        stop=(z == PASSES - 1),
                    )
                result = keep.tile([P, m1 - m0], F32, name="result%d_%d" % (b, m0))
                if m0 == 0:
                    nc.scalar.copy(out=result[:], in_=acc[:])
                else:
                    nc.vector.tensor_copy(out=result[:], in_=acc[:])
                nc.sync.dma_start(out=out[b * P : (b + 1) * P, m0:m1], in_=result[:])

        wovens = [weigh(b) for b in range(BLOCKS - 1)]
        for b in range(BLOCKS - 1):
            finish(b, wovens[b])
        finish(BLOCKS - 1, weigh(BLOCKS - 1))
